import numpy as np
import ml_dtypes


def mxq(x, axis, fmt="e4m3"):
    dtype, down = {"e4m3": (ml_dtypes.float8_e4m3fn, 7), "e5m2": (ml_dtypes.float8_e5m2, 14)}[fmt]
    v = np.moveaxis(np.asarray(x, np.float32).astype(ml_dtypes.bfloat16).astype(np.float64), axis, -1)
    blocks = v.reshape(v.shape[:-1] + (-1, 32))
    amax = np.abs(blocks).max(-1, keepdims=True)
    byte = np.maximum(np.where(amax > 0, np.frexp(amax)[1] - 1 + 127, 0) - down, 1)
    scale = np.exp2(byte - 127.0)
    codes = (blocks / scale).astype(np.float32).astype(dtype).astype(np.float64)
    return np.moveaxis((codes * scale).reshape(v.shape), -1, axis)


WIDE = False


def mx_kscale(k):
    if not WIDE:
        return np.ones(k)
    levels = np.array([10, -10, 5, -5, 0])
    if k % 512:
        return np.exp2(np.random.permutation(np.resize(levels, k // 32))).repeat(32)
    a = np.empty((k // 512, 16))
    for p in range(k // 512):
        a[p, :8] = np.random.permutation(np.resize(levels, 8))
        for g in range(8):
            far = levels[np.abs(levels - a[p, g]) >= 10]
            a[p, g + 8] = far[np.random.randint(len(far))]
    return np.exp2(a.ravel()).repeat(32)


def f64(x):
    return np.asarray(x).astype(np.float64)


def striped(idx):
    return np.tile(idx.reshape(-1, 16).T, (8, 1)).astype(np.uint16)


def unstriped(offs):
    return offs[:16].T.reshape(-1).astype(np.int64)


def striped8(idx):
    return np.concatenate([x.reshape(-1, 16).T for x in idx]).astype(np.uint16)


def runs(offs, k):
    lists = np.stack([offs[16 * r : 16 * r + 16].T.reshape(-1) for r in range(8)]).astype(np.int64)
    return lists[np.arange(k) % 512 // 64]


def pack_weight(w):
    k, n = w.shape
    w = f64(np.asarray(w, np.float32).astype(ml_dtypes.bfloat16)).reshape(k // 32, 32, n)
    amax = np.abs(w).max(1)
    byte = np.clip(np.where(amax > 0, np.frexp(amax)[1] - 1 + 127 - 7, 1), 1, 254)
    scaled = (w * np.exp2(127.0 - byte)[:, None, :]).reshape(k, n).astype(np.float32)
    words = np.ascontiguousarray(scaled.reshape(k // 512, 128, 4, n).transpose(0, 1, 3, 2)).astype(ml_dtypes.float8_e4m3fn).view(np.uint8)
    return words, np.ascontiguousarray(byte.astype(np.uint8).reshape(k // 512, 16, n))


def unpack_weight(words, scales):
    g, p, n, _ = words.shape
    vals = np.ascontiguousarray(words).view(ml_dtypes.float8_e4m3fn).astype(np.float64) * np.repeat(np.exp2(scales.astype(np.float64) - 127.0), 8, axis=1)[..., None]
    return vals.transpose(0, 1, 3, 2).reshape(g * 512, n)


E2M1 = np.array([0.0, 0.5, 1.0, 1.5, 2.0, 3.0, 4.0, 6.0, -0.0, -0.5, -1.0, -1.5, -2.0, -3.0, -4.0, -6.0])


def pack_fp4(w):
    k, n = w.shape
    w = f64(np.asarray(w, np.float32).astype(ml_dtypes.bfloat16)).reshape(k // 32, 32, n)
    amax = np.abs(w).max(1)
    mant, ex = np.frexp(amax / 6.0)
    byte = np.clip(np.where(amax > 0, np.where(mant > 0.5, ex, ex - 1) + 127, 1), 1, 254)
    scaled = (w * np.exp2(127.0 - byte)[:, None, :]).reshape(k, n).astype(np.float32)
    c = np.ascontiguousarray(scaled.reshape(k // 512, 128, 4, n).transpose(0, 1, 3, 2)).astype(ml_dtypes.float4_e2m1fn).view(np.uint8) & 0xF
    words = (c[..., 0::2] | (c[..., 1::2] << 4)).reshape(k // 512, 128, 2 * n)
    return np.ascontiguousarray(words), np.ascontiguousarray(byte.astype(np.uint8).reshape(k // 512, 16, n))


def unpack_fp4(words, scales):
    g, _, n = scales.shape
    words = np.ascontiguousarray(words).reshape(g, 128, n, 2)
    nib = np.empty((g, 128, n, 4), np.uint8)
    nib[..., 0::2] = words & 0xF
    nib[..., 1::2] = words >> 4
    vals = E2M1[nib] * np.repeat(np.exp2(scales.astype(np.float64) - 127.0), 8, axis=1)[..., None]
    return vals.transpose(0, 1, 3, 2).reshape(g * 512, n)


def sigmoid(v):
    return 1.0 / (1.0 + np.exp(-np.maximum(v, -700.0)))

def planes(y):
    n, m = y.shape
    v = y.astype(np.float32).astype(ml_dtypes.bfloat16).astype(np.float64).reshape(n // 32, 32, m)
    top = np.abs(v).max(1)
    byte = np.clip(np.where(top > 0, np.frexp(top)[1] - 1 + 127 - 7, 1), 1, 254)
    codes = (v * np.exp2(127.0 - byte)[:, None, :]).reshape(n, m).astype(np.float32).astype(ml_dtypes.float8_e4m3fn).view(np.uint8)
    words = codes.reshape(n // 512, 128, 4, m).transpose(0, 1, 3, 2)
    return np.ascontiguousarray(words), np.ascontiguousarray(byte.astype(np.uint8).reshape(n // 512, 16, m))


K, T, S, H = 512, 2048, 512, 512


def setup_inputs():
    n = np.random.standard_normal
    s = mx_kscale(K)[:, None]
    u = mx_kscale(S)
    packed_xT = pack_weight(n((K, T)) * s)
    packed_w1 = pack_fp4(n((K, H)) / np.sqrt(K) / s)
    return {
        "x_words": packed_xT[0],
        "x_scales": packed_xT[1],
        "w1_words": packed_w1[0],
        "w1_scales": packed_w1[1],
        "tau": np.random.uniform(0.3, 0.9, (H, 1)).astype(np.float32),
        "sl": np.random.uniform(1.0, 2.0, (H, 1)).astype(np.float32),
        "th": (0.5 * n((H, 1))).astype(np.float32),
        "ga": (np.random.uniform(0.5, 1.5, (H, 1)) * u[:, None]).astype(np.float32),
        "gb": (np.random.uniform(0.5, 1.5, (H, 1)) / u[:, None]).astype(np.float32),
        "sl2": np.random.uniform(1.5, 3.0, (S, 1)).astype(np.float32),
        "th2": (0.5 * n((S, 1))).astype(np.float32),
        "offs": striped(np.random.permutation(T)[:S]),
        "n1": striped(np.random.permutation(S)),
        "n2": striped(np.random.permutation(S)),
        "n3": striped8(np.stack([np.random.permutation(S) for _ in range(8)])),
        "n4": striped8(np.stack([np.random.permutation(S) for _ in range(8)])),
        "n5": striped8(np.stack([np.random.permutation(S) for _ in range(8)])),
        "n6": striped8(np.stack([np.random.permutation(S) for _ in range(8)])),
    }


def reference(x_words, x_scales, w1_words, w1_scales, tau, sl, th, ga, gb, sl2, th2, offs, n1, n2, n3, n4, n5, n6):
    xq = unpack_weight(x_words, x_scales)[:, unstriped(offs)]
    y = unpack_fp4(w1_words, w1_scales).T @ xq
    sq = (y) ** 2
    ea = np.exp(-1.0 * (f64(tau) * sq[:, unstriped(n1)]))
    z = f64(ga) * (y * ea - (0.5 * y[:, unstriped(n2)]))
    pa = y[np.arange(H)[:, None], runs(n3, H)]
    sg = sigmoid(f64(sl) * (y[np.arange(H)[:, None], runs(n4, H)] - f64(th)))
    z2 = f64(gb) * (pa + sg * (y - pa))
    s = 0.0625 * ((mxq(z, 0, "e4m3").T @ mxq(z2, 0, "e4m3")))
    sg2 = sigmoid(f64(sl2) * (s[np.arange(S)[:, None], runs(n5, S)] - f64(th2)))
    out_0 = 1.5 * (s * (sg2 - (sg2[np.arange(S)[:, None], runs(n6, S)])))
    return (out_0,) + planes(out_0)

@@ -1,0 +1,261 @@
+from contextlib import ExitStack
+
+import concourse.mybir as mybir
+
+F32 = mybir.dt.float32
+BF16 = mybir.dt.bfloat16
+I32 = mybir.dt.int32
+U32 = mybir.dt.uint32
+U16 = mybir.dt.uint16
+U8 = mybir.dt.uint8
+FP8X4 = mybir.dt.float8_e4m3fn_x4
+FP4X4 = mybir.dt.float4_e2m1fn_x4
+ACT = mybir.ActivationFunctionType
+ALU = mybir.AluOpType
+
+P = 128
+PACK = 4
+T = 2048
+S = 512
+HALF = 256
+PER_COL = 16
+HALVES = ((0, S),)
+WIN = 2 * S
+CHUNKS = ((0, 256), (256, 384), (384, 512))
+FLOPS = 2 * 2 * 512 * 512 * 512
+
+
+def entries(lst, lo, hi):
+    return lst[:, lo // PER_COL : hi // PER_COL]
+
+
+def tile_picked_selfegaebledb_none_po_kernel(
+    tc, x_words, x_scales, w1_words, w1_scales, tau, sl, th, ga, gb, sl2, th2,
+    offs, n1, n2, n3, n4, n5, n6, out_0, out_1, out_2,
+):
+    nc = tc.nc
+    with ExitStack() as ctx:
+        keep = ctx.enter_context(tc.tile_pool(name="keep", bufs=1))
+        psum = ctx.enter_context(tc.psum_pool(name="psum", bufs=1))
+
+        def load_list(src, name):
+            lst = keep.tile([P, S // PER_COL], U16, name=name)
+            nc.sync.dma_start(lst[:], src)
+            return lst
+
+        def load_rows(src, name, queue):
+            col = keep.tile([P, PACK], F32, name=name)
+            queue.dma_start(col[:], src.rearrange("(p t) o -> p (t o)", t=PACK))
+            return col
+
+        xs_win = keep.tile([P, T], U8, name="xs_win", align_bytes=64)
+        ws_raw = keep.tile([P, S], U8, name="ws_raw", align_bytes=64)
+        nc.vector.memset(xs_win[:].bitcast(I32), 0)
+        nc.gpsimd.memset(ws_raw[:].bitcast(I32), 0)
+
+        xs_rows = x_scales[0].bitcast(I32)
+        ws_rows = w1_scales[0].bitcast(I32)
+
+        def load_scale_rows(queue, dst, rows, q):
+            queue.dma_start(dst[32 * q : 32 * q + 4, :].bitcast(I32), rows[4 * q : 4 * q + 4, :])
+
+        offs_l = load_list(offs, "offs_l")
+        w_raw = keep.tile([P, 2 * S], U8, name="w_raw", align_bytes=64)
+        nc.sync.dma_start(w_raw[:].bitcast(I32), w1_words[0].bitcast(I32))
+        for q in range(4):
+            load_scale_rows(nc.sync, xs_win, xs_rows, q)
+        load_scale_rows(nc.sync, ws_raw, ws_rows, 0)
+        xw_win = keep.tile([P, T], I32, name="xw_win", align_bytes=64)
+        nc.sync.dma_start(xw_win[:], x_words[0].rearrange("p n t -> p (n t)").bitcast(I32))
+        for q in range(1, 4):
+            load_scale_rows(nc.sync, ws_raw, ws_rows, q)
+        tau_c = load_rows(tau, "tau_c", nc.sync)
+        n1_l = load_list(n1, "n1_l")
+        gb_c = load_rows(gb, "gb_c", nc.sync)
+        ga_c = load_rows(ga, "ga_c", nc.sync)
+        n3_l = load_list(n3, "n3_l")
+        n4_l = load_list(n4, "n4_l")
+        n2_l = load_list(n2, "n2_l")
+        n5_l = load_list(n5, "n5_l")
+        n6_l = load_list(n6, "n6_l")
+        sl_c = load_rows(sl, "sl_c", nc.sync)
+        th_c = load_rows(th, "th_c", nc.sync)
+        sl2_c = load_rows(sl2, "sl2_c", nc.sync)
+        th2_c = load_rows(th2, "th2_c", nc.sync)
+
+        def scaled(src, factor, name):
+            dst = keep.tile([P, PACK], F32, name=name)
+            nc.gpsimd.tensor_scalar(dst[:], src[:], factor, 0.0, ALU.mult, ALU.add)
+            return dst
+
+        def minus_product(a, b, name):
+            prod = keep.tile([P, PACK], F32, name=name + "_p")
+            nc.gpsimd.tensor_tensor(prod[:], a[:], b[:], ALU.mult)
+            return scaled(prod, -1.0, name)
+
+        neg_tau = keep.tile([P, PACK], F32, name="neg_tau")
+        nc.scalar.activation(neg_tau[:], tau_c[:], ACT.Copy, scale=-1.0)
+        neg_half_ga = scaled(ga_c, -0.5, "neg_half_ga")
+        bias1 = minus_product(sl_c, th_c, "bias1")
+        bias2 = minus_product(sl2_c, th2_c, "bias2")
+
+        w_dealt = keep.tile([P, 2 * S], U8, name="w_dealt", align_bytes=64)
+        ws_dealt = keep.tile([P, S], U8, name="ws_dealt", align_bytes=64)
+        nc.scalar.copy(
+            w_dealt[:].bitcast(U16).rearrange("p (t m) -> p t m", t=PACK),
+            w_raw[:].bitcast(U16).rearrange("p (m t) -> p t m", t=PACK),
+        )
+        xs_pick = keep.tile([P, S], U8, name="xs_pick", align_bytes=64)
+        xw_pick = keep.tile([P, S], U32, name="xw_pick", align_bytes=64)
+        nc.vector.tensor_copy(xs_pick[:], xs_win[:].indirect(offs_l[:]))
+        nc.vector.tensor_copy(
+            ws_dealt[:].rearrange("p (t m) -> p t m", t=PACK),
+            ws_raw[:].rearrange("p (m t) -> p t m", t=PACK),
+        )
+        nc.vector.tensor_copy(xw_pick[:], xw_win[:].bitcast(U32).indirect(offs_l[:]))
+
+        y_ps = []
+        for t in range(PACK):
+            bank = psum.tile([P, S], F32, name=f"y_ps{t}")
+            nc.tensor.matmul_mx(
+                out=bank[:],
+                lhsT=w_dealt[:, 2 * P * t : 2 * P * (t + 1)].bitcast(FP4X4),
+                lhsT_scale=ws_dealt[:, P * t : P * (t + 1)],
+                rhs=xw_pick[:].bitcast(FP8X4),
+                rhs_scale=xs_pick[:],
+                start=True,
+                stop=True,
+            )
+            y_ps.append(bank)
+
+        def col(c, t):
+            return c[:, t : t + 1]
+
+        sq = [keep.tile([P, WIN], F32, name=f"sq{t}", tag=f"sq{t}") for t in range(PACK)]
+        y = [keep.tile([P, WIN], F32, name=f"y{t}", tag=f"y{t}") for t in range(PACK)]
+        yb = [keep.tile([P, WIN], F32, name=f"yb{t}") for t in range(PACK)]
+        ya = [keep.tile([P, S], F32, name=f"ya{t}") for t in range(PACK)]
+        yb_all = keep.tile([P, PACK, S], F32, name="yb_all")
+        ea = keep.tile([P, PACK, S], F32, name="ea")
+        t1 = keep.tile([P, PACK, S], F32, name="t1")
+        gap = keep.tile([P, PACK, S], F32, name="gap")
+        pull = keep.tile([P, PACK, S], F32, name="pull")
+
+        def fetch_ea(t):
+            for lo, hi in HALVES:
+                nc.scalar.activation(ea[:, t, lo:hi], sq[t][:].indirect(entries(n1_l, lo, hi)), ACT.Exp, scale=col(neg_tau, t))
+
+        def square(t):
+            nc.scalar.activation(sq[t][:, :S], y_ps[t][:], ACT.Square)
+
+        square(0)
+        for t in (1, 0, 2, 3):
+            nc.vector.tensor_copy(y[t][:, :S], y_ps[t][:])
+            nc.vector.tensor_scalar(yb[t][:, :S], y[t][:, :S], col(gb_c, t), None, ALU.mult)
+            nc.sync.dma_start(yb_all[:, t, :], yb[t][:, :S])
+        fetch_ea(0)
+        square(1)
+        for t in range(1, PACK):
+            if t + 1 < PACK:
+                square(t + 1)
+            fetch_ea(t)
+        for t in range(PACK):
+            nc.vector.tensor_scalar(ya[t][:], y[t][:, :S], col(neg_half_ga, t), None, ALU.mult)
+        for t in range(PACK):
+            nc.vector.scalar_tensor_tensor(t1[:, t, :], y_ps[t][:], col(ga_c, t), ea[:, t, :], ALU.mult, ALU.mult)
+            for lo, hi in HALVES:
+                nc.vector.tensor_tensor(gap[:, t, lo:hi], yb[t][:].indirect(entries(n3_l, lo, hi)), yb_all[:, t, lo:hi], ALU.subtract)
+
+        sg = keep.tile([P, PACK, S], F32, name="sg", tag=f"sq{PACK - 1}")
+        for t in range(PACK):
+            for lo, hi in HALVES:
+                nc.scalar.activation(sg[:, t, lo:hi], y[t][:].indirect(entries(n4_l, lo, hi)), ACT.Sigmoid, bias=col(bias1, t), scale=col(sl_c, t))
+            nc.vector.scalar_tensor_tensor(pull[:, t, :], sg[:, t, :], -1.0, gap[:, t, :], ALU.add, ALU.mult)
+
+        z2_bf = keep.tile([P, PACK * S], BF16, name="z2_bf", align_bytes=64)
+        nc.vector.tensor_tensor(
+            z2_bf[:].rearrange("p (c i t) -> p c t i", i=PACK, t=PACK),
+            yb_all[:].rearrange("p t (c i) -> p c t i", i=PACK),
+            pull[:].rearrange("p t (c i) -> p c t i", i=PACK),
+            ALU.subtract,
+        )
+        z2_codes = keep.tile([P, S], U32, name="z2_codes", align_bytes=64)
+        z2_scales = keep.tile([P, S], U8, name="z2_scales", align_bytes=64)
+        nc.vector.quantize_mx(out=z2_codes[:].bitcast(FP8X4), scales=z2_scales[:], in_=z2_bf[:])
+
+        z_bf = keep.tile([P, PACK * S], BF16, name="z_bf", align_bytes=64)
+        z_view = z_bf[:].rearrange("p (i m t) -> p m t i", i=PACK, t=PACK)
+        t1_view = t1[:].rearrange("p t (m i) -> p m t i", i=PACK)
+        for c, (lo, hi) in enumerate(CHUNKS):
+            far = keep.tile([P, PACK, hi - lo], F32, name=f"far{c}", tag=f"y{PACK - 2 - c}")
+            for t in range(PACK):
+                nc.scalar.activation(far[:, t, :], ya[t][:].indirect(entries(n2_l, lo, hi)), ACT.Copy)
+            nc.vector.tensor_tensor(
+                z_view[:, lo // PACK : hi // PACK],
+                t1_view[:, lo // PACK : hi // PACK],
+                far[:].rearrange("p t (m i) -> p m t i", i=PACK),
+                ALU.add,
+            )
+
+        s_sb = []
+        for t in range(PACK):
+            z_codes = keep.tile([P, P], U32, name=f"z_codes{t}", align_bytes=64)
+            z_scales = keep.tile([P, P], U8, name=f"z_scales{t}", align_bytes=64)
+            nc.vector.quantize_mx(out=z_codes[:].bitcast(FP8X4), scales=z_scales[:], in_=z_bf[:, S * t : S * (t + 1)])
+            bank = psum.tile([P, S], F32, name=f"s_ps{t}")
+            nc.tensor.matmul_mx(
+                out=bank[:],
+                lhsT=z_codes[:].bitcast(FP8X4),
+                lhsT_scale=z_scales[:],
+                rhs=z2_codes[:].bitcast(FP8X4),
+                rhs_scale=z2_scales[:],
+                start=True,
+                stop=True,
+            )
+            s_sb.append((bank, keep.tile([P, WIN], F32, name=f"s{t}")))
+        nc.scalar.activation(s_sb[0][1][:, :S], s_sb[0][0][:], ACT.Copy, scale=0.0625)
+        for bank, dst in s_sb[1:]:
+            nc.vector.tensor_scalar(dst[:, :S], bank[:], 0.0625, None, ALU.mult)
+        s = [dst for bank, dst in s_sb]
+
+        sg2 = [keep.tile([P, WIN if t < PACK - 1 else S], F32, name=f"sg2_{t}") for t in range(PACK)]
+        other = keep.tile([P, PACK, S], F32, name="other")
+        diff = keep.tile([P, PACK, S], F32, name="diff")
+        res = keep.tile([P, PACK, S], F32, name="res")
+        out_rows = out_0.rearrange("(p t) c -> p t c", t=PACK)
+
+        def fetch_sg2(t):
+            for lo, hi in HALVES:
+                nc.scalar.activation(sg2[t][:, lo:hi], s[t][:].indirect(entries(n5_l, lo, hi)), ACT.Sigmoid, bias=col(bias2, t), scale=col(sl2_c, t))
+
+        def finish(t, lo, hi, parts):
+            for a, b in parts:
+                nc.scalar.activation(other[:, t, a:b], sg2[t][:].indirect(entries(n6_l, a, b)), ACT.Copy)
+            nc.vector.tensor_tensor(diff[:, t, lo:hi], sg2[t][:, lo:hi], other[:, t, lo:hi], ALU.subtract)
+            nc.vector.scalar_tensor_tensor(res[:, t, lo:hi], diff[:, t, lo:hi], 1.5, s[t][:, lo:hi], ALU.mult, ALU.mult)
+            nc.sync.dma_start(out_rows[:, t, lo:hi], res[:, t, lo:hi])
+
+        fetch_sg2(0)
+        fetch_sg2(1)
+        finish(0, 0, S, HALVES)
+        fetch_sg2(2)
+        finish(1, 0, S, HALVES)
+        finish(2, 0, S, HALVES)
+        fetch_sg2(3)
+
+        o_codes = keep.tile([P, S], U32, name="o_codes", align_bytes=64)
+        o_scales = keep.tile([P, S], U8, name="o_scales", align_bytes=64)
+        words_out = out_1[0].rearrange("p n t -> p (n t)").bitcast(I32)
+        for c, (lo, hi) in enumerate(CHUNKS):
+            finish(PACK - 1, lo, hi, ((lo, hi),))
+            o_bf = keep.tile([P, PACK * (hi - lo)], BF16, name=f"o_bf{c}", align_bytes=64)
+            nc.vector.tensor_copy(
+                o_bf[:].rearrange("p (c i t) -> p c t i", i=PACK, t=PACK),
+                res[:, :, lo:hi].rearrange("p t (c i) -> p c t i", i=PACK),
+            )
+            nc.vector.quantize_mx(out=o_codes[:, lo:hi].bitcast(FP8X4), scales=o_scales[:, lo:hi], in_=o_bf[:])
+            nc.sync.dma_start(words_out[:, lo:hi], o_codes[:, lo:hi].bitcast(I32))
+        scales_out = out_2[0].bitcast(I32)
+        for q in range(4):
+            queue = nc.scalar if q % 2 else nc.sync
+            queue.dma_start(scales_out[4 * q : 4 * q + 4, :], o_scales[32 * q : 32 * q + 4, :].bitcast(I32))

@@ -21,7 +21,8 @@ HALF = 256
 PER_COL = 16
 HALVES = ((0, S),)
 WIN = 2 * S
-CHUNKS = ((0, 256), (256, 384), (384, 512))
+CHUNKS = ((0, 384), (384, 512))
+TWO = ((0, HALF), (HALF, S))
 FLOPS = 2 * 2 * 512 * 512 * 512
 
 
@@ -49,7 +50,7 @@ def tile_picked_selfegaebledb_none_po_kernel(
             return col
 
         xs_win = keep.tile([P, T], U8, name="xs_win", align_bytes=64)
-        ws_raw = keep.tile([P, S], U8, name="ws_raw", align_bytes=64)
+        ws_raw = keep.tile([P, S], U8, name="ws_raw", tag="ws_raw", align_bytes=64)
         nc.vector.memset(xs_win[:].bitcast(I32), 0)
         nc.gpsimd.memset(ws_raw[:].bitcast(I32), 0)
 
@@ -68,65 +69,64 @@ def tile_picked_selfegaebledb_none_po_kernel(
         xw_win = keep.tile([P, T], I32, name="xw_win", align_bytes=64)
         nc.sync.dma_start(xw_win[:], x_words[0].rearrange("p n t -> p (n t)").bitcast(I32))
         for q in range(1, 4):
-            load_scale_rows(nc.sync, ws_raw, ws_rows, q)
+            load_scale_rows(nc.sync if q < 2 else nc.gpsimd, ws_raw, ws_rows, q)
         tau_c = load_rows(tau, "tau_c", nc.sync)
         n1_l = load_list(n1, "n1_l")
         gb_c = load_rows(gb, "gb_c", nc.sync)
         ga_c = load_rows(ga, "ga_c", nc.sync)
         n3_l = load_list(n3, "n3_l")
-        n4_l = load_list(n4, "n4_l")
-        n2_l = load_list(n2, "n2_l")
-        n5_l = load_list(n5, "n5_l")
-        n6_l = load_list(n6, "n6_l")
         sl_c = load_rows(sl, "sl_c", nc.sync)
         th_c = load_rows(th, "th_c", nc.sync)
+        n4_l = load_list(n4, "n4_l")
+        n2_l = load_list(n2, "n2_l")
         sl2_c = load_rows(sl2, "sl2_c", nc.sync)
         th2_c = load_rows(th2, "th2_c", nc.sync)
+        n5_l = load_list(n5, "n5_l")
+        n6_l = load_list(n6, "n6_l")
 
-        def scaled(src, factor, name):
-            dst = keep.tile([P, PACK], F32, name=name)
+        def scaled(src, factor, name, tag):
+            dst = keep.tile([P, PACK], F32, name=name, tag=tag)
             nc.gpsimd.tensor_scalar(dst[:], src[:], factor, 0.0, ALU.mult, ALU.add)
             return dst
 
-        def minus_product(a, b, name):
+        def minus_product(a, b, name, tag):
             prod = keep.tile([P, PACK], F32, name=name + "_p")
             nc.gpsimd.tensor_tensor(prod[:], a[:], b[:], ALU.mult)
-            return scaled(prod, -1.0, name)
+            return scaled(prod, -1.0, name, tag)
 
-        neg_tau = keep.tile([P, PACK], F32, name="neg_tau")
-        nc.scalar.activation(neg_tau[:], tau_c[:], ACT.Copy, scale=-1.0)
-        neg_half_ga = scaled(ga_c, -0.5, "neg_half_ga")
-        bias1 = minus_product(sl_c, th_c, "bias1")
-        bias2 = minus_product(sl2_c, th2_c, "bias2")
+        neg_tau = scaled(tau_c, -1.0, "neg_tau", "rate")
+        neg_half_ga = scaled(ga_c, -0.5, "neg_half_ga", "neg_half_ga")
+        bias2 = minus_product(sl2_c, th2_c, "bias2", "bias2")
 
         w_dealt = keep.tile([P, 2 * S], U8, name="w_dealt", align_bytes=64)
         ws_dealt = keep.tile([P, S], U8, name="ws_dealt", align_bytes=64)
-        nc.scalar.copy(
-            w_dealt[:].bitcast(U16).rearrange("p (t m) -> p t m", t=PACK),
-            w_raw[:].bitcast(U16).rearrange("p (m t) -> p t m", t=PACK),
-        )
+        for t in range(PACK):
+            nc.scalar.copy(
+                w_dealt[:].bitcast(U16)[:, P * t : P * (t + 1)],
+                w_raw[:].bitcast(U16).rearrange("p (m t) -> p t m", t=PACK)[:, t, :],
+            )
         xs_pick = keep.tile([P, S], U8, name="xs_pick", align_bytes=64)
-        xw_pick = keep.tile([P, S], U32, name="xw_pick", align_bytes=64)
         nc.vector.tensor_copy(xs_pick[:], xs_win[:].indirect(offs_l[:]))
         nc.vector.tensor_copy(
             ws_dealt[:].rearrange("p (t m) -> p t m", t=PACK),
             ws_raw[:].rearrange("p (m t) -> p t m", t=PACK),
         )
-        nc.vector.tensor_copy(xw_pick[:], xw_win[:].bitcast(U32).indirect(offs_l[:]))
-
-        y_ps = []
-        for t in range(PACK):
-            bank = psum.tile([P, S], F32, name=f"y_ps{t}")
-            nc.tensor.matmul_mx(
-                out=bank[:],
-                lhsT=w_dealt[:, 2 * P * t : 2 * P * (t + 1)].bitcast(FP4X4),
-                lhsT_scale=ws_dealt[:, P * t : P * (t + 1)],
-                rhs=xw_pick[:].bitcast(FP8X4),
-                rhs_scale=xs_pick[:],
-                start=True,
-                stop=True,
-            )
-            y_ps.append(bank)
+        xw_pick = keep.tile([P, S], U32, name="xw_pick", tag="ws_raw", align_bytes=64)
+        y_ps = [psum.tile([P, S], F32, name=f"y_ps{t}", tag=f"y_ps{t}") for t in range(PACK)]
+        for lo, hi in TWO:
+            nc.vector.tensor_copy(xw_pick[:, lo:hi], xw_win[:].bitcast(U32).indirect(entries(offs_l, lo, hi)))
+        for h, t in ((0, 0), (0, 1), (1, 0), (1, 1), (0, 2), (1, 2), (0, 3), (1, 3)):
+            lo, hi = TWO[h]
+            if True:
+                nc.tensor.matmul_mx(
+                    out=y_ps[t][:, lo:hi],
+                    lhsT=w_dealt[:, 2 * P * t : 2 * P * (t + 1)].bitcast(FP4X4),
+                    lhsT_scale=ws_dealt[:, P * t : P * (t + 1)],
+                    rhs=xw_pick[:, lo:hi].bitcast(FP8X4),
+                    rhs_scale=xs_pick[:, lo:hi],
+                    start=True,
+                    stop=True,
+                )
 
         def col(c, t):
             return c[:, t : t + 1]
@@ -136,42 +136,46 @@ def tile_picked_selfegaebledb_none_po_kernel(
         yb = [keep.tile([P, WIN], F32, name=f"yb{t}") for t in range(PACK)]
         ya = [keep.tile([P, S], F32, name=f"ya{t}") for t in range(PACK)]
         yb_all = keep.tile([P, PACK, S], F32, name="yb_all")
-        ea = keep.tile([P, PACK, S], F32, name="ea")
+        ea = [keep.tile([P, S], F32, name=f"ea{t}") for t in range(PACK)]
         t1 = keep.tile([P, PACK, S], F32, name="t1")
-        gap = keep.tile([P, PACK, S], F32, name="gap")
+        gap = [keep.tile([P, S], F32, name=f"gap{t}") for t in range(PACK)]
         pull = keep.tile([P, PACK, S], F32, name="pull")
 
         def fetch_ea(t):
             for lo, hi in HALVES:
-                nc.scalar.activation(ea[:, t, lo:hi], sq[t][:].indirect(entries(n1_l, lo, hi)), ACT.Exp, scale=col(neg_tau, t))
+                nc.scalar.activation(ea[t][:, lo:hi], sq[t][:].indirect(entries(n1_l, lo, hi)), ACT.Exp, scale=col(neg_tau, t))
 
         def square(t):
             nc.scalar.activation(sq[t][:, :S], y_ps[t][:], ACT.Square)
 
         square(0)
-        for t in (1, 0, 2, 3):
-            nc.vector.tensor_copy(y[t][:, :S], y_ps[t][:])
-            nc.vector.tensor_scalar(yb[t][:, :S], y[t][:, :S], col(gb_c, t), None, ALU.mult)
-            nc.sync.dma_start(yb_all[:, t, :], yb[t][:, :S])
+        for pair in ((1, 0), (2, 3)):
+            for t in pair:
+                nc.vector.tensor_copy(y[t][:, :S], y_ps[t][:])
+            for t in pair:
+                nc.vector.tensor_scalar(yb[t][:, :S], y[t][:, :S], col(gb_c, t), None, ALU.mult)
+                nc.sync.dma_start(yb_all[:, t, :], yb[t][:, :S])
         fetch_ea(0)
         square(1)
         for t in range(1, PACK):
             if t + 1 < PACK:
                 square(t + 1)
             fetch_ea(t)
-        for t in range(PACK):
+        for t in range(PACK - 1):
             nc.vector.tensor_scalar(ya[t][:], y[t][:, :S], col(neg_half_ga, t), None, ALU.mult)
         for t in range(PACK):
-            nc.vector.scalar_tensor_tensor(t1[:, t, :], y_ps[t][:], col(ga_c, t), ea[:, t, :], ALU.mult, ALU.mult)
+            nc.vector.scalar_tensor_tensor(t1[:, t, :], y_ps[t][:], col(ga_c, t), ea[t][:], ALU.mult, ALU.mult)
             for lo, hi in HALVES:
-                nc.vector.tensor_tensor(gap[:, t, lo:hi], yb[t][:].indirect(entries(n3_l, lo, hi)), yb_all[:, t, lo:hi], ALU.subtract)
+                nc.vector.tensor_tensor(gap[t][:, lo:hi], yb[t][:].indirect(entries(n3_l, lo, hi)), yb_all[:, t, lo:hi], ALU.subtract)
 
-        sg = keep.tile([P, PACK, S], F32, name="sg", tag=f"sq{PACK - 1}")
+        bias1 = minus_product(sl_c, th_c, "bias1", "rate")
+        sg = [keep.tile([P, S], F32, name=f"sg{t}") for t in range(PACK)]
         for t in range(PACK):
             for lo, hi in HALVES:
-                nc.scalar.activation(sg[:, t, lo:hi], y[t][:].indirect(entries(n4_l, lo, hi)), ACT.Sigmoid, bias=col(bias1, t), scale=col(sl_c, t))
-            nc.vector.scalar_tensor_tensor(pull[:, t, :], sg[:, t, :], -1.0, gap[:, t, :], ALU.add, ALU.mult)
+                nc.scalar.activation(sg[t][:, lo:hi], y[t][:].indirect(entries(n4_l, lo, hi)), ACT.Sigmoid, bias=col(bias1, t), scale=col(sl_c, t))
+            nc.vector.scalar_tensor_tensor(pull[:, t, :], sg[t][:], -1.0, gap[t][:], ALU.add, ALU.mult)
 
+        nc.scalar.activation(ya[PACK - 1][:], y_ps[PACK - 1][:], ACT.Copy, scale=col(neg_half_ga, PACK - 1))
         z2_bf = keep.tile([P, PACK * S], BF16, name="z2_bf", align_bytes=64)
         nc.vector.tensor_tensor(
             z2_bf[:].rearrange("p (c i t) -> p c t i", i=PACK, t=PACK),
@@ -197,63 +201,75 @@ def tile_picked_selfegaebledb_none_po_kernel(
                 ALU.add,
             )
 
-        s_sb = []
+        s = [keep.tile([P, WIN], F32, name=f"s{t}") for t in range(PACK)]
+        s_ps = []
         for t in range(PACK):
             z_codes = keep.tile([P, P], U32, name=f"z_codes{t}", align_bytes=64)
             z_scales = keep.tile([P, P], U8, name=f"z_scales{t}", align_bytes=64)
             nc.vector.quantize_mx(out=z_codes[:].bitcast(FP8X4), scales=z_scales[:], in_=z_bf[:, S * t : S * (t + 1)])
-            bank = psum.tile([P, S], F32, name=f"s_ps{t}")
-            nc.tensor.matmul_mx(
-                out=bank[:],
-                lhsT=z_codes[:].bitcast(FP8X4),
-                lhsT_scale=z_scales[:],
-                rhs=z2_codes[:].bitcast(FP8X4),
-                rhs_scale=z2_scales[:],
-                start=True,
-                stop=True,
-            )
-            s_sb.append((bank, keep.tile([P, WIN], F32, name=f"s{t}")))
-        nc.scalar.activation(s_sb[0][1][:, :S], s_sb[0][0][:], ACT.Copy, scale=0.0625)
-        for bank, dst in s_sb[1:]:
-            nc.vector.tensor_scalar(dst[:, :S], bank[:], 0.0625, None, ALU.mult)
-        s = [dst for bank, dst in s_sb]
+            for lo, hi in TWO if t == 0 else ((0, S),):
+                bank = psum.tile([P, hi - lo], F32, name=f"s_ps{t}_{lo}", tag="y_ps0" if lo > 0 else f"s_ps{t}")
+                nc.tensor.matmul_mx(
+                    out=bank[:],
+                    lhsT=z_codes[:].bitcast(FP8X4),
+                    lhsT_scale=z_scales[:],
+                    rhs=z2_codes[:, lo:hi].bitcast(FP8X4),
+                    rhs_scale=z2_scales[:, lo:hi],
+                    start=True,
+                    stop=True,
+                )
+                s_ps.append((t, lo, hi, bank))
+        for t, lo, hi, bank in s_ps:
+            if t == 0:
+                nc.scalar.activation(s[t][:, lo:hi], bank[:], ACT.Copy, scale=0.0625)
+            else:
+                nc.vector.tensor_scalar(s[t][:, lo:hi], bank[:], 0.0625, None, ALU.mult)
 
-        sg2 = [keep.tile([P, WIN if t < PACK - 1 else S], F32, name=f"sg2_{t}") for t in range(PACK)]
-        other = keep.tile([P, PACK, S], F32, name="other")
-        diff = keep.tile([P, PACK, S], F32, name="diff")
-        res = keep.tile([P, PACK, S], F32, name="res")
-        out_rows = out_0.rearrange("(p t) c -> p t c", t=PACK)
+        sg2 = [keep.tile([P, WIN], F32, name=f"sg2_{t}") for t in range(PACK)]
+        other = [keep.tile([P, S], F32, name=f"other{t}") for t in range(PACK)]
+        diff = [keep.tile([P, S], F32, name=f"diff{t}") for t in range(PACK)]
+        res = keep.tile([P, 2, PACK, HALF], F32, name="res")
+        out_rows = out_0.rearrange("(p t) (h c) -> p t h c", t=PACK, h=2)
+
+        def halves(ap):
+            return ap.rearrange("p (h c) -> p h c", c=HALF)
 
         def fetch_sg2(t):
-            for lo, hi in HALVES:
-                nc.scalar.activation(sg2[t][:, lo:hi], s[t][:].indirect(entries(n5_l, lo, hi)), ACT.Sigmoid, bias=col(bias2, t), scale=col(sl2_c, t))
+            nc.scalar.activation(sg2[t][:, :S], s[t][:].indirect(n5_l[:]), ACT.Sigmoid, bias=col(bias2, t), scale=col(sl2_c, t))
 
-        def finish(t, lo, hi, parts):
-            for a, b in parts:
-                nc.scalar.activation(other[:, t, a:b], sg2[t][:].indirect(entries(n6_l, a, b)), ACT.Copy)
-            nc.vector.tensor_tensor(diff[:, t, lo:hi], sg2[t][:, lo:hi], other[:, t, lo:hi], ALU.subtract)
-            nc.vector.scalar_tensor_tensor(res[:, t, lo:hi], diff[:, t, lo:hi], 1.5, s[t][:, lo:hi], ALU.mult, ALU.mult)
-            nc.sync.dma_start(out_rows[:, t, lo:hi], res[:, t, lo:hi])
+        def finish(t, lo, hi):
+            h = slice(lo // HALF, hi // HALF)
+            nc.scalar.activation(other[t][:, lo:hi], sg2[t][:].indirect(entries(n6_l, lo, hi)), ACT.Copy)
+            nc.vector.tensor_tensor(diff[t][:, lo:hi], sg2[t][:, lo:hi], other[t][:, lo:hi], ALU.subtract)
+            nc.vector.scalar_tensor_tensor(res[:, h, t, :], halves(diff[t][:, lo:hi]), 1.5, halves(s[t][:, lo:hi]), ALU.mult, ALU.mult)
+            nc.sync.dma_start(out_rows[:, t, h, :], res[:, h, t, :])
 
         fetch_sg2(0)
         fetch_sg2(1)
-        finish(0, 0, S, HALVES)
+        finish(0, 0, S)
         fetch_sg2(2)
-        finish(1, 0, S, HALVES)
-        finish(2, 0, S, HALVES)
+        finish(1, 0, S)
+        finish(2, 0, S)
         fetch_sg2(3)
 
         o_codes = keep.tile([P, S], U32, name="o_codes", align_bytes=64)
         o_scales = keep.tile([P, S], U8, name="o_scales", align_bytes=64)
         words_out = out_1[0].rearrange("p n t -> p (n t)").bitcast(I32)
-        for c, (lo, hi) in enumerate(CHUNKS):
-            finish(PACK - 1, lo, hi, ((lo, hi),))
-            o_bf = keep.tile([P, PACK * (hi - lo)], BF16, name=f"o_bf{c}", align_bytes=64)
-            nc.vector.tensor_copy(
-                o_bf[:].rearrange("p (c i t) -> p c t i", i=PACK, t=PACK),
-                res[:, :, lo:hi].rearrange("p t (c i) -> p c t i", i=PACK),
-            )
-            nc.vector.quantize_mx(out=o_codes[:, lo:hi].bitcast(FP8X4), scales=o_scales[:, lo:hi], in_=o_bf[:])
+        o_bf = []
+        for lo, hi in TWO:
+            finish(PACK - 1, lo, hi)
+        for h in range(2):
+            half_bf = keep.tile([P, PACK * HALF], BF16, name=f"o_bf{h}", align_bytes=64)
+            dst = half_bf[:].rearrange("p (c i t) -> p c t i", i=PACK, t=PACK)
+            src = res[:, h].rearrange("p t (c i) -> p c t i", i=PACK)
+            if h == 0:
+                nc.scalar.copy(dst, src)
+            else:
+                nc.vector.tensor_copy(dst, src)
+            o_bf.append(half_bf)
+        for h in (1, 0):
+            lo, hi = TWO[h]
+            nc.vector.quantize_mx(out=o_codes[:, lo:hi].bitcast(FP8X4), scales=o_scales[:, lo:hi], in_=o_bf[h][:])
             nc.sync.dma_start(words_out[:, lo:hi], o_codes[:, lo:hi].bitcast(I32))
         scales_out = out_2[0].bitcast(I32)
         for q in range(4):

@@ -49,7 +49,7 @@ def tile_picked_selfegaebledb_none_po_kernel(
             queue.dma_start(col[:], src.rearrange("(p t) o -> p (t o)", t=PACK))
             return col
 
-        xs_win = keep.tile([P, T], U8, name="xs_win", align_bytes=64)
+        xs_win = keep.tile([P, T], U8, name="xs_win", tag="xs_win")
         ws_raw = keep.tile([P, S], U8, name="ws_raw", tag="ws_raw", align_bytes=64)
         nc.vector.memset(xs_win[:].bitcast(I32), 0)
         nc.gpsimd.memset(ws_raw[:].bitcast(I32), 0)
@@ -61,7 +61,7 @@ def tile_picked_selfegaebledb_none_po_kernel(
             queue.dma_start(dst[32 * q : 32 * q + 4, :].bitcast(I32), rows[4 * q : 4 * q + 4, :])
 
         offs_l = load_list(offs, "offs_l")
-        w_raw = keep.tile([P, 2 * S], U8, name="w_raw", align_bytes=64)
+        w_raw = keep.tile([P, 2 * S], U8, name="w_raw", tag="w_raw")
         nc.sync.dma_start(w_raw[:].bitcast(I32), w1_words[0].bitcast(I32))
         for q in range(4):
             load_scale_rows(nc.sync, xs_win, xs_rows, q)
@@ -69,7 +69,7 @@ def tile_picked_selfegaebledb_none_po_kernel(
         xw_win = keep.tile([P, T], I32, name="xw_win", align_bytes=64)
         nc.sync.dma_start(xw_win[:], x_words[0].rearrange("p n t -> p (n t)").bitcast(I32))
         for q in range(1, 4):
-            load_scale_rows(nc.sync if q < 2 else nc.gpsimd, ws_raw, ws_rows, q)
+            load_scale_rows(nc.sync, ws_raw, ws_rows, q)
         tau_c = load_rows(tau, "tau_c", nc.sync)
         n1_l = load_list(n1, "n1_l")
         gb_c = load_rows(gb, "gb_c", nc.sync)
@@ -86,17 +86,13 @@ def tile_picked_selfegaebledb_none_po_kernel(
 
         def scaled(src, factor, name, tag):
             dst = keep.tile([P, PACK], F32, name=name, tag=tag)
-            nc.gpsimd.tensor_scalar(dst[:], src[:], factor, 0.0, ALU.mult, ALU.add)
+            nc.scalar.activation(dst[:], src[:], ACT.Copy, scale=factor)
             return dst
 
         def minus_product(a, b, name, tag):
-            prod = keep.tile([P, PACK], F32, name=name + "_p")
-            nc.gpsimd.tensor_tensor(prod[:], a[:], b[:], ALU.mult)
-            return scaled(prod, -1.0, name, tag)
-
-        neg_tau = scaled(tau_c, -1.0, "neg_tau", "rate")
-        neg_half_ga = scaled(ga_c, -0.5, "neg_half_ga", "neg_half_ga")
-        bias2 = minus_product(sl2_c, th2_c, "bias2", "bias2")
+            dst = keep.tile([P, PACK], F32, name=name, tag=tag)
+            nc.vector.scalar_tensor_tensor(dst[:], a[:], -1.0, b[:], ALU.mult, ALU.mult)
+            return dst
 
         w_dealt = keep.tile([P, 2 * S], U8, name="w_dealt", align_bytes=64)
         ws_dealt = keep.tile([P, S], U8, name="ws_dealt", align_bytes=64)
@@ -105,6 +101,7 @@ def tile_picked_selfegaebledb_none_po_kernel(
                 w_dealt[:].bitcast(U16)[:, P * t : P * (t + 1)],
                 w_raw[:].bitcast(U16).rearrange("p (m t) -> p t m", t=PACK)[:, t, :],
             )
+        neg_tau = scaled(tau_c, -1.0, "neg_tau", "w_raw")
         xs_pick = keep.tile([P, S], U8, name="xs_pick", align_bytes=64)
         nc.vector.tensor_copy(xs_pick[:], xs_win[:].indirect(offs_l[:]))
         nc.vector.tensor_copy(
@@ -128,6 +125,8 @@ def tile_picked_selfegaebledb_none_po_kernel(
                     stop=True,
                 )
 
+        neg_half_ga = scaled(ga_c, -0.5, "neg_half_ga", "xs_win")
+
         def col(c, t):
             return c[:, t : t + 1]
 
@@ -136,7 +135,7 @@ def tile_picked_selfegaebledb_none_po_kernel(
         yb = [keep.tile([P, WIN], F32, name=f"yb{t}") for t in range(PACK)]
         ya = [keep.tile([P, S], F32, name=f"ya{t}") for t in range(PACK)]
         yb_all = keep.tile([P, PACK, S], F32, name="yb_all")
-        ea = [keep.tile([P, S], F32, name=f"ea{t}") for t in range(PACK)]
+        ea = [keep.tile([P, S], F32, name=f"ea{t}", tag=f"ea{t}") for t in range(PACK)]
         t1 = keep.tile([P, PACK, S], F32, name="t1")
         gap = [keep.tile([P, S], F32, name=f"gap{t}") for t in range(PACK)]
         pull = keep.tile([P, PACK, S], F32, name="pull")
@@ -149,7 +148,7 @@ def tile_picked_selfegaebledb_none_po_kernel(
             nc.scalar.activation(sq[t][:, :S], y_ps[t][:], ACT.Square)
 
         square(0)
-        for pair in ((1, 0), (2, 3)):
+        for pair in ((1, 0, 2, 3),):
             for t in pair:
                 nc.vector.tensor_copy(y[t][:, :S], y_ps[t][:])
             for t in pair:
@@ -168,7 +167,7 @@ def tile_picked_selfegaebledb_none_po_kernel(
             for lo, hi in HALVES:
                 nc.vector.tensor_tensor(gap[t][:, lo:hi], yb[t][:].indirect(entries(n3_l, lo, hi)), yb_all[:, t, lo:hi], ALU.subtract)
 
-        bias1 = minus_product(sl_c, th_c, "bias1", "rate")
+        bias1 = minus_product(sl_c, th_c, "bias1", "ea1")
         sg = [keep.tile([P, S], F32, name=f"sg{t}") for t in range(PACK)]
         for t in range(PACK):
             for lo, hi in HALVES:
@@ -176,11 +175,12 @@ def tile_picked_selfegaebledb_none_po_kernel(
             nc.vector.scalar_tensor_tensor(pull[:, t, :], sg[t][:], -1.0, gap[t][:], ALU.add, ALU.mult)
 
         nc.scalar.activation(ya[PACK - 1][:], y_ps[PACK - 1][:], ACT.Copy, scale=col(neg_half_ga, PACK - 1))
+        bias2 = minus_product(sl2_c, th2_c, "bias2", "ea3")
         z2_bf = keep.tile([P, PACK * S], BF16, name="z2_bf", align_bytes=64)
         nc.vector.tensor_tensor(
-            z2_bf[:].rearrange("p (c i t) -> p c t i", i=PACK, t=PACK),
-            yb_all[:].rearrange("p t (c i) -> p c t i", i=PACK),
-            pull[:].rearrange("p t (c i) -> p c t i", i=PACK),
+            z2_bf[:].rearrange("p (c i t) -> p c t i", i=2, t=PACK),
+            yb_all[:].rearrange("p t (c i) -> p c t i", i=2),
+            pull[:].rearrange("p t (c i) -> p c t i", i=2),
             ALU.subtract,
         )
         z2_codes = keep.tile([P, S], U32, name="z2_codes", align_bytes=64)
@@ -260,8 +260,9 @@ def tile_picked_selfegaebledb_none_po_kernel(
             finish(PACK - 1, lo, hi)
         for h in range(2):
             half_bf = keep.tile([P, PACK * HALF], BF16, name=f"o_bf{h}", align_bytes=64)
-            dst = half_bf[:].rearrange("p (c i t) -> p c t i", i=PACK, t=PACK)
-            src = res[:, h].rearrange("p t (c i) -> p c t i", i=PACK)
+            run = 2 if h == 0 else PACK
+            dst = half_bf[:].rearrange("p (c i t) -> p c t i", i=run, t=PACK)
+            src = res[:, h].rearrange("p t (c i) -> p c t i", i=run)
             if h == 0:
                 nc.scalar.copy(dst, src)
             else:

@@ -152,29 +152,31 @@ def tile_picked_selfegaebledb_none_po_kernel(
             for t in pair:
                 nc.vector.tensor_copy(y[t][:, :S], y_ps[t][:])
             for t in pair:
-                nc.vector.tensor_scalar(yb[t][:, :S], y[t][:, :S], col(gb_c, t), None, ALU.mult)
-                nc.sync.dma_start(yb_all[:, t, :], yb[t][:, :S])
+                nc.gpsimd.tensor_scalar(yb[t][:, :S], y[t][:, :S], col(gb_c, t), 0.0, ALU.mult, ALU.add)
+                if t != 1:
+                    nc.sync.dma_start(yb_all[:, t, :], yb[t][:, :S])
+        nc.vector.tensor_scalar(yb_all[:, 1, :], y_ps[1][:], col(gb_c, 1), None, ALU.mult)
+        for t in (3,):
+            nc.vector.tensor_tensor(sq[t][:, :S], y_ps[t][:], y[t][:, :S], ALU.mult)
         fetch_ea(0)
         square(1)
+        square(2)
         for t in range(1, PACK):
-            if t + 1 < PACK:
-                square(t + 1)
             fetch_ea(t)
-        for t in range(PACK - 1):
-            nc.vector.tensor_scalar(ya[t][:], y[t][:, :S], col(neg_half_ga, t), None, ALU.mult)
+        for t in range(PACK):
+            nc.gpsimd.tensor_scalar(ya[t][:], y[t][:, :S], col(neg_half_ga, t), 0.0, ALU.mult, ALU.add)
         for t in range(PACK):
             nc.vector.scalar_tensor_tensor(t1[:, t, :], y_ps[t][:], col(ga_c, t), ea[t][:], ALU.mult, ALU.mult)
-            for lo, hi in HALVES:
-                nc.vector.tensor_tensor(gap[t][:, lo:hi], yb[t][:].indirect(entries(n3_l, lo, hi)), yb_all[:, t, lo:hi], ALU.subtract)
+            u = (1, 0, 2, 3)[t]
+            nc.vector.tensor_tensor(gap[u][:], yb[u][:].indirect(n3_l[:]), yb_all[:, u, :], ALU.subtract)
 
-        bias1 = minus_product(sl_c, th_c, "bias1", "ea1")
+        bias1 = minus_product(sl_c, th_c, "bias1", "ea0")
         sg = [keep.tile([P, S], F32, name=f"sg{t}") for t in range(PACK)]
         for t in range(PACK):
             for lo, hi in HALVES:
                 nc.scalar.activation(sg[t][:, lo:hi], y[t][:].indirect(entries(n4_l, lo, hi)), ACT.Sigmoid, bias=col(bias1, t), scale=col(sl_c, t))
             nc.vector.scalar_tensor_tensor(pull[:, t, :], sg[t][:], -1.0, gap[t][:], ALU.add, ALU.mult)
 
-        nc.scalar.activation(ya[PACK - 1][:], y_ps[PACK - 1][:], ACT.Copy, scale=col(neg_half_ga, PACK - 1))
         bias2 = minus_product(sl2_c, th2_c, "bias2", "ea3")
         z2_bf = keep.tile([P, PACK * S], BF16, name="z2_bf", align_bytes=64)
         nc.vector.tensor_tensor(
@@ -268,7 +270,7 @@ def tile_picked_selfegaebledb_none_po_kernel(
             else:
                 nc.vector.tensor_copy(dst, src)
             o_bf.append(half_bf)
-        for h in (1, 0):
+        for h in (0, 1):
             lo, hi = TWO[h]
             nc.vector.quantize_mx(out=o_codes[:, lo:hi].bitcast(FP8X4), scales=o_scales[:, lo:hi], in_=o_bf[h][:])
             nc.sync.dma_start(words_out[:, lo:hi], o_codes[:, lo:hi].bitcast(I32))

@@ -15,19 +15,31 @@ ALU = mybir.AluOpType
 
 P = 128
 PACK = 4
+QUADRANTS = 4
 T = 2048
-S = 512
-HALF = 256
+N = 512
+HALF = N // 2
+HALVES = ((0, HALF), (HALF, N))
 PER_COL = 16
-HALVES = ((0, S),)
-WIN = 2 * S
-CHUNKS = ((0, 384), (384, 512))
-TWO = ((0, HALF), (HALF, S))
-FLOPS = 2 * 2 * 512 * 512 * 512
+WIN = 2 * N
+Z_PARTS = ((0, 384), (384, N))
+FLOPS = 2 * 2 * N * N * N
 
 
 def entries(lst, lo, hi):
     return lst[:, lo // PER_COL : hi // PER_COL]
+
+
+def col(vec, t):
+    return vec[:, t : t + 1]
+
+
+def side_by_side(rounded, run):
+    return rounded.rearrange("p (c i t) -> p c t i", i=run, t=PACK)
+
+
+def by_runs(row_tiles, run):
+    return row_tiles.rearrange("p t (c i) -> p c t i", i=run)
 
 
 def tile_picked_selfegaebledb_none_po_kernel(
@@ -40,47 +52,46 @@ def tile_picked_selfegaebledb_none_po_kernel(
         psum = ctx.enter_context(tc.psum_pool(name="psum", bufs=1))
 
         def load_list(src, name):
-            lst = keep.tile([P, S // PER_COL], U16, name=name)
+            lst = keep.tile([P, N // PER_COL], U16, name=name)
             nc.sync.dma_start(lst[:], src)
             return lst
 
-        def load_rows(src, name, queue):
-            col = keep.tile([P, PACK], F32, name=name)
-            queue.dma_start(col[:], src.rearrange("(p t) o -> p (t o)", t=PACK))
-            return col
+        def load_vector(src, name):
+            vec = keep.tile([P, PACK], F32, name=name)
+            nc.sync.dma_start(vec[:], src.rearrange("(p t) o -> p (t o)", t=PACK))
+            return vec
+
+        def load_scale_rows(dst, rows, q):
+            nc.sync.dma_start(dst[32 * q : 32 * q + 4, :].bitcast(I32), rows[4 * q : 4 * q + 4, :])
 
         xs_win = keep.tile([P, T], U8, name="xs_win", tag="xs_win")
-        ws_raw = keep.tile([P, S], U8, name="ws_raw", tag="ws_raw", align_bytes=64)
+        ws_raw = keep.tile([P, N], U8, name="ws_raw", tag="ws_raw", align_bytes=64)
         nc.vector.memset(xs_win[:].bitcast(I32), 0)
         nc.gpsimd.memset(ws_raw[:].bitcast(I32), 0)
-
         xs_rows = x_scales[0].bitcast(I32)
         ws_rows = w1_scales[0].bitcast(I32)
 
-        def load_scale_rows(queue, dst, rows, q):
-            queue.dma_start(dst[32 * q : 32 * q + 4, :].bitcast(I32), rows[4 * q : 4 * q + 4, :])
-
         offs_l = load_list(offs, "offs_l")
-        w_raw = keep.tile([P, 2 * S], U8, name="w_raw", tag="w_raw")
+        w_raw = keep.tile([P, 2 * N], U8, name="w_raw", tag="w_raw")
         nc.sync.dma_start(w_raw[:].bitcast(I32), w1_words[0].bitcast(I32))
-        for q in range(4):
-            load_scale_rows(nc.sync, xs_win, xs_rows, q)
-        load_scale_rows(nc.sync, ws_raw, ws_rows, 0)
+        for q in range(QUADRANTS):
+            load_scale_rows(xs_win, xs_rows, q)
+        load_scale_rows(ws_raw, ws_rows, 0)
         xw_win = keep.tile([P, T], I32, name="xw_win", align_bytes=64)
         nc.sync.dma_start(xw_win[:], x_words[0].rearrange("p n t -> p (n t)").bitcast(I32))
-        for q in range(1, 4):
-            load_scale_rows(nc.sync, ws_raw, ws_rows, q)
-        tau_c = load_rows(tau, "tau_c", nc.sync)
+        for q in range(1, QUADRANTS):
+            load_scale_rows(ws_raw, ws_rows, q)
+        tau_c = load_vector(tau, "tau_c")
         n1_l = load_list(n1, "n1_l")
-        gb_c = load_rows(gb, "gb_c", nc.sync)
-        ga_c = load_rows(ga, "ga_c", nc.sync)
+        gb_c = load_vector(gb, "gb_c")
+        ga_c = load_vector(ga, "ga_c")
         n3_l = load_list(n3, "n3_l")
-        sl_c = load_rows(sl, "sl_c", nc.sync)
-        th_c = load_rows(th, "th_c", nc.sync)
+        sl_c = load_vector(sl, "sl_c")
+        th_c = load_vector(th, "th_c")
         n4_l = load_list(n4, "n4_l")
         n2_l = load_list(n2, "n2_l")
-        sl2_c = load_rows(sl2, "sl2_c", nc.sync)
-        th2_c = load_rows(th2, "th2_c", nc.sync)
+        sl2_c = load_vector(sl2, "sl2_c")
+        th2_c = load_vector(th2, "th2_c")
         n5_l = load_list(n5, "n5_l")
         n6_l = load_list(n6, "n6_l")
 
@@ -94,113 +105,120 @@ def tile_picked_selfegaebledb_none_po_kernel(
             nc.vector.scalar_tensor_tensor(dst[:], a[:], -1.0, b[:], ALU.mult, ALU.mult)
             return dst
 
-        w_dealt = keep.tile([P, 2 * S], U8, name="w_dealt", align_bytes=64)
-        ws_dealt = keep.tile([P, S], U8, name="ws_dealt", align_bytes=64)
+        w_dealt = keep.tile([P, 2 * N], U8, name="w_dealt", align_bytes=64)
+        ws_dealt = keep.tile([P, N], U8, name="ws_dealt", align_bytes=64)
         for t in range(PACK):
             nc.scalar.copy(
                 w_dealt[:].bitcast(U16)[:, P * t : P * (t + 1)],
                 w_raw[:].bitcast(U16).rearrange("p (m t) -> p t m", t=PACK)[:, t, :],
             )
         neg_tau = scaled(tau_c, -1.0, "neg_tau", "w_raw")
-        xs_pick = keep.tile([P, S], U8, name="xs_pick", align_bytes=64)
+        xs_pick = keep.tile([P, N], U8, name="xs_pick", align_bytes=64)
         nc.vector.tensor_copy(xs_pick[:], xs_win[:].indirect(offs_l[:]))
         nc.vector.tensor_copy(
             ws_dealt[:].rearrange("p (t m) -> p t m", t=PACK),
             ws_raw[:].rearrange("p (m t) -> p t m", t=PACK),
         )
-        xw_pick = keep.tile([P, S], U32, name="xw_pick", tag="ws_raw", align_bytes=64)
-        y_ps = [psum.tile([P, S], F32, name=f"y_ps{t}", tag=f"y_ps{t}") for t in range(PACK)]
-        for lo, hi in TWO:
-            nc.vector.tensor_copy(xw_pick[:, lo:hi], xw_win[:].bitcast(U32).indirect(entries(offs_l, lo, hi)))
-        for h, t in ((0, 0), (0, 1), (1, 0), (1, 1), (0, 2), (1, 2), (0, 3), (1, 3)):
-            lo, hi = TWO[h]
-            if True:
-                nc.tensor.matmul_mx(
-                    out=y_ps[t][:, lo:hi],
-                    lhsT=w_dealt[:, 2 * P * t : 2 * P * (t + 1)].bitcast(FP4X4),
-                    lhsT_scale=ws_dealt[:, P * t : P * (t + 1)],
-                    rhs=xw_pick[:, lo:hi].bitcast(FP8X4),
-                    rhs_scale=xs_pick[:, lo:hi],
-                    start=True,
-                    stop=True,
-                )
+        xw_pick = [
+            keep.tile([P, HALF], U32, name="xw_pick0", align_bytes=64),
+            keep.tile([P, HALF], U32, name="xw_pick1", tag="ws_raw", align_bytes=64),
+        ]
+        y_ps = [psum.tile([P, N], F32, name=f"y_ps{t}", tag=f"y_ps{t}") for t in range(PACK)]
+        for h, (lo, hi) in enumerate(HALVES):
+            nc.vector.tensor_copy(xw_pick[h][:], xw_win[:].bitcast(U32).indirect(entries(offs_l, lo, hi)))
+
+        def first_product(t, h):
+            lo, hi = HALVES[h]
+            nc.tensor.matmul_mx(
+                out=y_ps[t][:, lo:hi],
+                lhsT=w_dealt[:, 2 * P * t : 2 * P * (t + 1)].bitcast(FP4X4),
+                lhsT_scale=ws_dealt[:, P * t : P * (t + 1)],
+                rhs=xw_pick[h][:].bitcast(FP8X4),
+                rhs_scale=xs_pick[:, lo:hi],
+                start=True,
+                stop=True,
+            )
+
+        for h in range(2):
+            for t in (0, 1):
+                first_product(t, h)
+        for t in (2, 3):
+            for h in range(2):
+                first_product(t, h)
 
         neg_half_ga = scaled(ga_c, -0.5, "neg_half_ga", "xs_win")
-
-        def col(c, t):
-            return c[:, t : t + 1]
 
         sq = [keep.tile([P, WIN], F32, name=f"sq{t}", tag=f"sq{t}") for t in range(PACK)]
         y = [keep.tile([P, WIN], F32, name=f"y{t}", tag=f"y{t}") for t in range(PACK)]
         yb = [keep.tile([P, WIN], F32, name=f"yb{t}") for t in range(PACK)]
-        ya = [keep.tile([P, S], F32, name=f"ya{t}") for t in range(PACK)]
-        yb_all = keep.tile([P, PACK, S], F32, name="yb_all")
-        ea = [keep.tile([P, S], F32, name=f"ea{t}", tag=f"ea{t}") for t in range(PACK)]
-        t1 = keep.tile([P, PACK, S], F32, name="t1")
-        gap = [keep.tile([P, S], F32, name=f"gap{t}") for t in range(PACK)]
-        pull = keep.tile([P, PACK, S], F32, name="pull")
+        ya = [keep.tile([P, N], F32, name=f"ya{t}") for t in range(PACK)]
+        yb_all = keep.tile([P, PACK, N], F32, name="yb_all")
+        ea = [keep.tile([P, N], F32, name=f"ea{t}", tag=f"ea{t}") for t in range(PACK)]
+        near = keep.tile([P, PACK, N], F32, name="near")
+        gap = [keep.tile([P, N], F32, name=f"gap{t}") for t in range(PACK)]
+        pull = keep.tile([P, PACK, N], F32, name="pull")
+
+        def scale_rows(dst, t, factor):
+            nc.gpsimd.tensor_scalar(dst, y[t][:, :N], col(factor, t), 0.0, ALU.mult, ALU.add)
+
+        def square_on_scalar(t):
+            nc.scalar.activation(sq[t][:, :N], y_ps[t][:], ACT.Square)
 
         def fetch_ea(t):
-            for lo, hi in HALVES:
-                nc.scalar.activation(ea[t][:, lo:hi], sq[t][:].indirect(entries(n1_l, lo, hi)), ACT.Exp, scale=col(neg_tau, t))
+            nc.scalar.activation(ea[t][:], sq[t][:].indirect(n1_l[:]), ACT.Exp, scale=col(neg_tau, t))
 
-        def square(t):
-            nc.scalar.activation(sq[t][:, :S], y_ps[t][:], ACT.Square)
+        def make_near(t):
+            nc.vector.scalar_tensor_tensor(near[:, t, :], y_ps[t][:], col(ga_c, t), ea[t][:], ALU.mult, ALU.mult)
 
-        square(0)
-        for pair in ((1, 0, 2, 3),):
-            for t in pair:
-                nc.vector.tensor_copy(y[t][:, :S], y_ps[t][:])
-            for t in pair:
-                nc.gpsimd.tensor_scalar(yb[t][:, :S], y[t][:, :S], col(gb_c, t), 0.0, ALU.mult, ALU.add)
-                if t != 1:
-                    nc.sync.dma_start(yb_all[:, t, :], yb[t][:, :S])
-        nc.vector.tensor_scalar(yb_all[:, 1, :], y_ps[1][:], col(gb_c, 1), None, ALU.mult)
-        for t in (3,):
-            nc.vector.tensor_tensor(sq[t][:, :S], y_ps[t][:], y[t][:, :S], ALU.mult)
+        def fetch_gap(t):
+            nc.vector.tensor_tensor(gap[t][:], yb[t][:].indirect(n3_l[:]), yb_all[:, t, :], ALU.subtract)
+
+        first, later = 1, (0, 2, 3)
+        square_on_scalar(0)
+        for t in (first, *later):
+            nc.vector.tensor_copy(y[t][:, :N], y_ps[t][:])
+        scale_rows(yb[first][:, :N], first, gb_c)
+        scale_rows(yb_all[:, first, :], first, gb_c)
+        for t in later:
+            scale_rows(yb[t][:, :N], t, gb_c)
+            nc.sync.dma_start(yb_all[:, t, :], yb[t][:, :N])
+        for t in (2, 3):
+            nc.vector.tensor_tensor(sq[t][:, :N], y_ps[t][:], y[t][:, :N], ALU.mult)
         fetch_ea(0)
-        square(1)
-        square(2)
+        square_on_scalar(1)
         for t in range(1, PACK):
             fetch_ea(t)
         for t in range(PACK):
-            nc.gpsimd.tensor_scalar(ya[t][:], y[t][:, :S], col(neg_half_ga, t), 0.0, ALU.mult, ALU.add)
-        for t in range(PACK):
-            nc.vector.scalar_tensor_tensor(t1[:, t, :], y_ps[t][:], col(ga_c, t), ea[t][:], ALU.mult, ALU.mult)
-            u = (1, 0, 2, 3)[t]
-            nc.vector.tensor_tensor(gap[u][:], yb[u][:].indirect(n3_l[:]), yb_all[:, u, :], ALU.subtract)
+            scale_rows(ya[t][:], t, neg_half_ga)
+        make_near(0)
+        fetch_gap(first)
+        for t in range(1, PACK):
+            make_near(t)
+        for t in later:
+            fetch_gap(t)
 
         bias1 = minus_product(sl_c, th_c, "bias1", "ea0")
-        sg = [keep.tile([P, S], F32, name=f"sg{t}") for t in range(PACK)]
+        sg = [keep.tile([P, N], F32, name=f"sg{t}") for t in range(PACK)]
         for t in range(PACK):
-            for lo, hi in HALVES:
-                nc.scalar.activation(sg[t][:, lo:hi], y[t][:].indirect(entries(n4_l, lo, hi)), ACT.Sigmoid, bias=col(bias1, t), scale=col(sl_c, t))
+            nc.scalar.activation(sg[t][:], y[t][:].indirect(n4_l[:]), ACT.Sigmoid, bias=col(bias1, t), scale=col(sl_c, t))
             nc.vector.scalar_tensor_tensor(pull[:, t, :], sg[t][:], -1.0, gap[t][:], ALU.add, ALU.mult)
 
         bias2 = minus_product(sl2_c, th2_c, "bias2", "ea3")
-        z2_bf = keep.tile([P, PACK * S], BF16, name="z2_bf", align_bytes=64)
-        nc.vector.tensor_tensor(
-            z2_bf[:].rearrange("p (c i t) -> p c t i", i=2, t=PACK),
-            yb_all[:].rearrange("p t (c i) -> p c t i", i=2),
-            pull[:].rearrange("p t (c i) -> p c t i", i=2),
-            ALU.subtract,
-        )
-        z2_codes = keep.tile([P, S], U32, name="z2_codes", align_bytes=64)
-        z2_scales = keep.tile([P, S], U8, name="z2_scales", align_bytes=64)
+        z2_bf = keep.tile([P, PACK * N], BF16, name="z2_bf", align_bytes=64)
+        nc.vector.tensor_tensor(side_by_side(z2_bf[:], 2), by_runs(yb_all[:], 2), by_runs(pull[:], 2), ALU.subtract)
+        z2_codes = keep.tile([P, N], U32, name="z2_codes", align_bytes=64)
+        z2_scales = keep.tile([P, N], U8, name="z2_scales", align_bytes=64)
         nc.vector.quantize_mx(out=z2_codes[:].bitcast(FP8X4), scales=z2_scales[:], in_=z2_bf[:])
 
-        z_bf = keep.tile([P, PACK * S], BF16, name="z_bf", align_bytes=64)
-        z_view = z_bf[:].rearrange("p (i m t) -> p m t i", i=PACK, t=PACK)
-        t1_view = t1[:].rearrange("p t (m i) -> p m t i", i=PACK)
-        for c, (lo, hi) in enumerate(CHUNKS):
-            far = keep.tile([P, PACK, hi - lo], F32, name=f"far{c}", tag=f"y{PACK - 2 - c}")
+        z_bf = keep.tile([P, PACK * N], BF16, name="z_bf", align_bytes=64)
+        z_dealt = z_bf[:].rearrange("p (i m t) -> p m t i", i=PACK, t=PACK)
+        near_walk = by_runs(near[:], PACK)
+        for c, (lo, hi) in enumerate(Z_PARTS):
+            far = keep.tile([P, PACK, hi - lo], F32, name=f"far{c}", tag=("y2", "y1")[c])
             for t in range(PACK):
                 nc.scalar.activation(far[:, t, :], ya[t][:].indirect(entries(n2_l, lo, hi)), ACT.Copy)
             nc.vector.tensor_tensor(
-                z_view[:, lo // PACK : hi // PACK],
-                t1_view[:, lo // PACK : hi // PACK],
-                far[:].rearrange("p t (m i) -> p m t i", i=PACK),
-                ALU.add,
+                z_dealt[:, lo // PACK : hi // PACK], near_walk[:, lo // PACK : hi // PACK], by_runs(far[:], PACK), ALU.add
             )
 
         s = [keep.tile([P, WIN], F32, name=f"s{t}") for t in range(PACK)]
@@ -208,8 +226,8 @@ def tile_picked_selfegaebledb_none_po_kernel(
         for t in range(PACK):
             z_codes = keep.tile([P, P], U32, name=f"z_codes{t}", align_bytes=64)
             z_scales = keep.tile([P, P], U8, name=f"z_scales{t}", align_bytes=64)
-            nc.vector.quantize_mx(out=z_codes[:].bitcast(FP8X4), scales=z_scales[:], in_=z_bf[:, S * t : S * (t + 1)])
-            for lo, hi in TWO if t == 0 else ((0, S),):
+            nc.vector.quantize_mx(out=z_codes[:].bitcast(FP8X4), scales=z_scales[:], in_=z_bf[:, N * t : N * (t + 1)])
+            for lo, hi in HALVES if t == 0 else ((0, N),):
                 bank = psum.tile([P, hi - lo], F32, name=f"s_ps{t}_{lo}", tag="y_ps0" if lo > 0 else f"s_ps{t}")
                 nc.tensor.matmul_mx(
                     out=bank[:],
@@ -228,53 +246,48 @@ def tile_picked_selfegaebledb_none_po_kernel(
                 nc.vector.tensor_scalar(s[t][:, lo:hi], bank[:], 0.0625, None, ALU.mult)
 
         sg2 = [keep.tile([P, WIN], F32, name=f"sg2_{t}") for t in range(PACK)]
-        other = [keep.tile([P, S], F32, name=f"other{t}") for t in range(PACK)]
-        diff = [keep.tile([P, S], F32, name=f"diff{t}") for t in range(PACK)]
+        other = [keep.tile([P, N], F32, name=f"other{t}") for t in range(PACK)]
+        diff = [keep.tile([P, N], F32, name=f"diff{t}") for t in range(PACK)]
         res = keep.tile([P, 2, PACK, HALF], F32, name="res")
         out_rows = out_0.rearrange("(p t) (h c) -> p t h c", t=PACK, h=2)
 
-        def halves(ap):
+        def in_halves(ap):
             return ap.rearrange("p (h c) -> p h c", c=HALF)
 
         def fetch_sg2(t):
-            nc.scalar.activation(sg2[t][:, :S], s[t][:].indirect(n5_l[:]), ACT.Sigmoid, bias=col(bias2, t), scale=col(sl2_c, t))
+            nc.scalar.activation(sg2[t][:, :N], s[t][:].indirect(n5_l[:]), ACT.Sigmoid, bias=col(bias2, t), scale=col(sl2_c, t))
 
         def finish(t, lo, hi):
-            h = slice(lo // HALF, hi // HALF)
+            hs = slice(lo // HALF, hi // HALF)
             nc.scalar.activation(other[t][:, lo:hi], sg2[t][:].indirect(entries(n6_l, lo, hi)), ACT.Copy)
             nc.vector.tensor_tensor(diff[t][:, lo:hi], sg2[t][:, lo:hi], other[t][:, lo:hi], ALU.subtract)
-            nc.vector.scalar_tensor_tensor(res[:, h, t, :], halves(diff[t][:, lo:hi]), 1.5, halves(s[t][:, lo:hi]), ALU.mult, ALU.mult)
-            nc.sync.dma_start(out_rows[:, t, h, :], res[:, h, t, :])
+            nc.vector.scalar_tensor_tensor(
+                res[:, hs, t, :], in_halves(diff[t][:, lo:hi]), 1.5, in_halves(s[t][:, lo:hi]), ALU.mult, ALU.mult
+            )
+            nc.sync.dma_start(out_rows[:, t, hs, :], res[:, hs, t, :])
 
         fetch_sg2(0)
         fetch_sg2(1)
-        finish(0, 0, S)
+        finish(0, 0, N)
         fetch_sg2(2)
-        finish(1, 0, S)
-        finish(2, 0, S)
+        finish(1, 0, N)
+        finish(2, 0, N)
         fetch_sg2(3)
 
-        o_codes = keep.tile([P, S], U32, name="o_codes", align_bytes=64)
-        o_scales = keep.tile([P, S], U8, name="o_scales", align_bytes=64)
+        o_codes = keep.tile([P, N], U32, name="o_codes", align_bytes=64)
+        o_scales = keep.tile([P, N], U8, name="o_scales", align_bytes=64)
         words_out = out_1[0].rearrange("p n t -> p (n t)").bitcast(I32)
-        o_bf = []
-        for lo, hi in TWO:
+        for lo, hi in HALVES:
             finish(PACK - 1, lo, hi)
-        for h in range(2):
-            half_bf = keep.tile([P, PACK * HALF], BF16, name=f"o_bf{h}", align_bytes=64)
-            run = 2 if h == 0 else PACK
-            dst = half_bf[:].rearrange("p (c i t) -> p c t i", i=run, t=PACK)
-            src = res[:, h].rearrange("p t (c i) -> p c t i", i=run)
-            if h == 0:
-                nc.scalar.copy(dst, src)
-            else:
-                nc.vector.tensor_copy(dst, src)
-            o_bf.append(half_bf)
-        for h in (0, 1):
-            lo, hi = TWO[h]
-            nc.vector.quantize_mx(out=o_codes[:, lo:hi].bitcast(FP8X4), scales=o_scales[:, lo:hi], in_=o_bf[h][:])
+
+        o_bf0 = keep.tile([P, PACK * HALF], BF16, name="o_bf0", align_bytes=64)
+        nc.scalar.copy(side_by_side(o_bf0[:], 2), by_runs(res[:, 0], 2))
+        o_bf1 = keep.tile([P, PACK * HALF], BF16, name="o_bf1", align_bytes=64)
+        nc.vector.tensor_copy(side_by_side(o_bf1[:], PACK), by_runs(res[:, 1], PACK))
+        for rounded, (lo, hi) in zip((o_bf0, o_bf1), HALVES):
+            nc.vector.quantize_mx(out=o_codes[:, lo:hi].bitcast(FP8X4), scales=o_scales[:, lo:hi], in_=rounded[:])
             nc.sync.dma_start(words_out[:, lo:hi], o_codes[:, lo:hi].bitcast(I32))
         scales_out = out_2[0].bitcast(I32)
-        for q in range(4):
+        for q in range(QUADRANTS):
             queue = nc.scalar if q % 2 else nc.sync
             queue.dma_start(scales_out[4 * q : 4 * q + 4, :], o_scales[32 * q : 32 * q + 4, :].bitcast(I32))

from contextlib import ExitStack

import concourse.mybir as mybir

F32 = mybir.dt.float32
BF16 = mybir.dt.bfloat16
I32 = mybir.dt.int32
U32 = mybir.dt.uint32
U16 = mybir.dt.uint16
U8 = mybir.dt.uint8
FP8X4 = mybir.dt.float8_e4m3fn_x4
FP4X4 = mybir.dt.float4_e2m1fn_x4
ACT = mybir.ActivationFunctionType
ALU = mybir.AluOpType

P = 128
PACK = 4
QUADRANTS = 4
T = 2048
N = 512
HALF = N // 2
HALVES = ((0, HALF), (HALF, N))
PER_COL = 16
WIN = 2 * N
Z_PARTS = ((0, 384), (384, N))
FLOPS = 2 * 2 * N * N * N


def entries(lst, lo, hi):
    return lst[:, lo // PER_COL : hi // PER_COL]


def col(vec, t):
    return vec[:, t : t + 1]


def side_by_side(rounded, run):
    return rounded.rearrange("p (c i t) -> p c t i", i=run, t=PACK)


def by_runs(row_tiles, run):
    return row_tiles.rearrange("p t (c i) -> p c t i", i=run)


def tile_picked_selfegaebledb_none_po_kernel(
    tc, x_words, x_scales, w1_words, w1_scales, tau, sl, th, ga, gb, sl2, th2,
    offs, n1, n2, n3, n4, n5, n6, out_0, out_1, out_2,
):
    nc = tc.nc
    with ExitStack() as ctx:
        keep = ctx.enter_context(tc.tile_pool(name="keep", bufs=1))
        psum = ctx.enter_context(tc.psum_pool(name="psum", bufs=1))

        def load_list(src, name):
            lst = keep.tile([P, N // PER_COL], U16, name=name)
            nc.sync.dma_start(lst[:], src)
            return lst

        def load_vector(src, name):
            vec = keep.tile([P, PACK], F32, name=name)
            nc.sync.dma_start(vec[:], src.rearrange("(p t) o -> p (t o)", t=PACK))
            return vec

        def load_scale_rows(dst, rows, q):
            nc.sync.dma_start(dst[32 * q : 32 * q + 4, :].bitcast(I32), rows[4 * q : 4 * q + 4, :])

        xs_win = keep.tile([P, T], U8, name="xs_win", tag="xs_win")
        ws_raw = keep.tile([P, N], U8, name="ws_raw", tag="ws_raw", align_bytes=64)
        nc.vector.memset(xs_win[:].bitcast(I32), 0)
        nc.gpsimd.memset(ws_raw[:].bitcast(I32), 0)
        xs_rows = x_scales[0].bitcast(I32)
        ws_rows = w1_scales[0].bitcast(I32)

        offs_l = load_list(offs, "offs_l")
        w_raw = keep.tile([P, 2 * N], U8, name="w_raw", tag="w_raw")
        nc.sync.dma_start(w_raw[:].bitcast(I32), w1_words[0].bitcast(I32))
        for q in range(QUADRANTS):
            load_scale_rows(xs_win, xs_rows, q)
        load_scale_rows(ws_raw, ws_rows, 0)
        xw_win = keep.tile([P, T], I32, name="xw_win", align_bytes=64)
        nc.sync.dma_start(xw_win[:], x_words[0].rearrange("p n t -> p (n t)").bitcast(I32))
        for q in range(1, QUADRANTS):
            load_scale_rows(ws_raw, ws_rows, q)
        tau_c = load_vector(tau, "tau_c")
        n1_l = load_list(n1, "n1_l")
        gb_c = load_vector(gb, "gb_c")
        ga_c = load_vector(ga, "ga_c")
        n3_l = load_list(n3, "n3_l")
        sl_c = load_vector(sl, "sl_c")
        th_c = load_vector(th, "th_c")
        n4_l = load_list(n4, "n4_l")
        n2_l = load_list(n2, "n2_l")
        sl2_c = load_vector(sl2, "sl2_c")
        th2_c = load_vector(th2, "th2_c")
        n5_l = load_list(n5, "n5_l")
        n6_l = load_list(n6, "n6_l")

        def scaled(src, factor, name, tag):
            dst = keep.tile([P, PACK], F32, name=name, tag=tag)
            nc.scalar.activation(dst[:], src[:], ACT.Copy, scale=factor)
            return dst

        def minus_product(a, b, name, tag):
            dst = keep.tile([P, PACK], F32, name=name, tag=tag)
            nc.vector.scalar_tensor_tensor(dst[:], a[:], -1.0, b[:], ALU.mult, ALU.mult)
            return dst

        w_dealt = keep.tile([P, 2 * N], U8, name="w_dealt", align_bytes=64)
        ws_dealt = keep.tile([P, N], U8, name="ws_dealt", align_bytes=64)
        for t in range(PACK):
            nc.scalar.copy(
                w_dealt[:].bitcast(U16)[:, P * t : P * (t + 1)],
                w_raw[:].bitcast(U16).rearrange("p (m t) -> p t m", t=PACK)[:, t, :],
            )
        neg_tau = scaled(tau_c, -1.0, "neg_tau", "w_raw")
        xs_pick = keep.tile([P, N], U8, name="xs_pick", align_bytes=64)
        nc.vector.tensor_copy(xs_pick[:], xs_win[:].indirect(offs_l[:]))
        nc.vector.tensor_copy(
            ws_dealt[:].rearrange("p (t m) -> p t m", t=PACK),
            ws_raw[:].rearrange("p (m t) -> p t m", t=PACK),
        )
        xw_pick = [
            keep.tile([P, HALF], U32, name="xw_pick0", align_bytes=64),
            keep.tile([P, HALF], U32, name="xw_pick1", tag="ws_raw", align_bytes=64),
        ]
        y_ps = [psum.tile([P, N], F32, name=f"y_ps{t}", tag=f"y_ps{t}") for t in range(PACK)]
        for h, (lo, hi) in enumerate(HALVES):
            nc.vector.tensor_copy(xw_pick[h][:], xw_win[:].bitcast(U32).indirect(entries(offs_l, lo, hi)))

        def first_product(t, h):
            lo, hi = HALVES[h]
            nc.tensor.matmul_mx(
                out=y_ps[t][:, lo:hi],
                lhsT=w_dealt[:, 2 * P * t : 2 * P * (t + 1)].bitcast(FP4X4),
                lhsT_scale=ws_dealt[:, P * t : P * (t + 1)],
                rhs=xw_pick[h][:].bitcast(FP8X4),
                rhs_scale=xs_pick[:, lo:hi],
                start=True,
                stop=True,
            )

        for h in range(2):
            for t in (0, 1):
                first_product(t, h)
        for t in (2, 3):
            for h in range(2):
                first_product(t, h)

        neg_half_ga = scaled(ga_c, -0.5, "neg_half_ga", "xs_win")

        sq = [keep.tile([P, WIN], F32, name=f"sq{t}", tag=f"sq{t}") for t in range(PACK)]
        y = [keep.tile([P, WIN], F32, name=f"y{t}", tag=f"y{t}") for t in range(PACK)]
        yb = [keep.tile([P, WIN], F32, name=f"yb{t}") for t in range(PACK)]
        ya = [keep.tile([P, N], F32, name=f"ya{t}") for t in range(PACK)]
        yb_all = keep.tile([P, PACK, N], F32, name="yb_all")
        ea = [keep.tile([P, N], F32, name=f"ea{t}", tag=f"ea{t}") for t in range(PACK)]
        near = keep.tile([P, PACK, N], F32, name="near")
        gap = [keep.tile([P, N], F32, name=f"gap{t}") for t in range(PACK)]
        pull = keep.tile([P, PACK, N], F32, name="pull")

        def scale_rows(dst, t, factor):
            nc.gpsimd.tensor_scalar(dst, y[t][:, :N], col(factor, t), 0.0, ALU.mult, ALU.add)

        def square_on_scalar(t):
            nc.scalar.activation(sq[t][:, :N], y_ps[t][:], ACT.Square)

        def fetch_ea(t):
            nc.scalar.activation(ea[t][:], sq[t][:].indirect(n1_l[:]), ACT.Exp, scale=col(neg_tau, t))

        def make_near(t):
            nc.vector.scalar_tensor_tensor(near[:, t, :], y_ps[t][:], col(ga_c, t), ea[t][:], ALU.mult, ALU.mult)

        def fetch_gap(t):
            nc.vector.tensor_tensor(gap[t][:], yb[t][:].indirect(n3_l[:]), yb_all[:, t, :], ALU.subtract)

        first, later = 1, (0, 2, 3)
        square_on_scalar(0)
        for t in (first, *later):
            nc.vector.tensor_copy(y[t][:, :N], y_ps[t][:])
        scale_rows(yb[first][:, :N], first, gb_c)
        scale_rows(yb_all[:, first, :], first, gb_c)
        for t in later:
            scale_rows(yb[t][:, :N], t, gb_c)
            nc.sync.dma_start(yb_all[:, t, :], yb[t][:, :N])
        for t in (2, 3):
            nc.vector.tensor_tensor(sq[t][:, :N], y_ps[t][:], y[t][:, :N], ALU.mult)
        fetch_ea(0)
        square_on_scalar(1)
        for t in range(1, PACK):
            fetch_ea(t)
        for t in range(PACK):
            scale_rows(ya[t][:], t, neg_half_ga)
        make_near(0)
        fetch_gap(first)
        for t in range(1, PACK):
            make_near(t)
        for t in later:
            fetch_gap(t)

        bias1 = minus_product(sl_c, th_c, "bias1", "ea0")
        sg = [keep.tile([P, N], F32, name=f"sg{t}") for t in range(PACK)]
        for t in range(PACK):
            nc.scalar.activation(sg[t][:], y[t][:].indirect(n4_l[:]), ACT.Sigmoid, bias=col(bias1, t), scale=col(sl_c, t))
            nc.vector.scalar_tensor_tensor(pull[:, t, :], sg[t][:], -1.0, gap[t][:], ALU.add, ALU.mult)

        bias2 = minus_product(sl2_c, th2_c, "bias2", "ea3")
        z2_bf = keep.tile([P, PACK * N], BF16, name="z2_bf", align_bytes=64)
        nc.vector.tensor_tensor(side_by_side(z2_bf[:], 2), by_runs(yb_all[:], 2), by_runs(pull[:], 2), ALU.subtract)
        z2_codes = keep.tile([P, N], U32, name="z2_codes", align_bytes=64)
        z2_scales = keep.tile([P, N], U8, name="z2_scales", align_bytes=64)
        nc.vector.quantize_mx(out=z2_codes[:].bitcast(FP8X4), scales=z2_scales[:], in_=z2_bf[:])

        z_bf = keep.tile([P, PACK * N], BF16, name="z_bf", align_bytes=64)
        z_dealt = z_bf[:].rearrange("p (i m t) -> p m t i", i=PACK, t=PACK)
        near_walk = by_runs(near[:], PACK)
        for c, (lo, hi) in enumerate(Z_PARTS):
            far = keep.tile([P, PACK, hi - lo], F32, name=f"far{c}", tag=("y2", "y1")[c])
            for t in range(PACK):
                nc.scalar.activation(far[:, t, :], ya[t][:].indirect(entries(n2_l, lo, hi)), ACT.Copy)
            nc.vector.tensor_tensor(
                z_dealt[:, lo // PACK : hi // PACK], near_walk[:, lo // PACK : hi // PACK], by_runs(far[:], PACK), ALU.add
            )

        s = [keep.tile([P, WIN], F32, name=f"s{t}") for t in range(PACK)]
        s_ps = []
        for t in range(PACK):
            z_codes = keep.tile([P, P], U32, name=f"z_codes{t}", align_bytes=64)
            z_scales = keep.tile([P, P], U8, name=f"z_scales{t}", align_bytes=64)
            nc.vector.quantize_mx(out=z_codes[:].bitcast(FP8X4), scales=z_scales[:], in_=z_bf[:, N * t : N * (t + 1)])
            for lo, hi in HALVES if t == 0 else ((0, N),):
                bank = psum.tile([P, hi - lo], F32, name=f"s_ps{t}_{lo}", tag="y_ps0" if lo > 0 else f"s_ps{t}")
                nc.tensor.matmul_mx(
                    out=bank[:],
                    lhsT=z_codes[:].bitcast(FP8X4),
                    lhsT_scale=z_scales[:],
                    rhs=z2_codes[:, lo:hi].bitcast(FP8X4),
                    rhs_scale=z2_scales[:, lo:hi],
                    start=True,
                    stop=True,
                )
                s_ps.append((t, lo, hi, bank))
        for t, lo, hi, bank in s_ps:
            if t == 0:
                nc.scalar.activation(s[t][:, lo:hi], bank[:], ACT.Copy, scale=0.0625)
            else:
                nc.vector.tensor_scalar(s[t][:, lo:hi], bank[:], 0.0625, None, ALU.mult)

        sg2 = [keep.tile([P, WIN], F32, name=f"sg2_{t}") for t in range(PACK)]
        other = [keep.tile([P, N], F32, name=f"other{t}") for t in range(PACK)]
        diff = [keep.tile([P, N], F32, name=f"diff{t}") for t in range(PACK)]
        res = keep.tile([P, 2, PACK, HALF], F32, name="res")
        out_rows = out_0.rearrange("(p t) (h c) -> p t h c", t=PACK, h=2)

        def in_halves(ap):
            return ap.rearrange("p (h c) -> p h c", c=HALF)

        def fetch_sg2(t):
            nc.scalar.activation(sg2[t][:, :N], s[t][:].indirect(n5_l[:]), ACT.Sigmoid, bias=col(bias2, t), scale=col(sl2_c, t))

        def finish(t, lo, hi):
            hs = slice(lo // HALF, hi // HALF)
            nc.scalar.activation(other[t][:, lo:hi], sg2[t][:].indirect(entries(n6_l, lo, hi)), ACT.Copy)
            nc.vector.tensor_tensor(diff[t][:, lo:hi], sg2[t][:, lo:hi], other[t][:, lo:hi], ALU.subtract)
            nc.vector.scalar_tensor_tensor(
                res[:, hs, t, :], in_halves(diff[t][:, lo:hi]), 1.5, in_halves(s[t][:, lo:hi]), ALU.mult, ALU.mult
            )
            nc.sync.dma_start(out_rows[:, t, hs, :], res[:, hs, t, :])

        fetch_sg2(0)
        fetch_sg2(1)
        finish(0, 0, N)
        fetch_sg2(2)
        finish(1, 0, N)
        finish(2, 0, N)
        fetch_sg2(3)

        o_codes = keep.tile([P, N], U32, name="o_codes", align_bytes=64)
        o_scales = keep.tile([P, N], U8, name="o_scales", align_bytes=64)
        words_out = out_1[0].rearrange("p n t -> p (n t)").bitcast(I32)
        for lo, hi in HALVES:
            finish(PACK - 1, lo, hi)

        o_bf0 = keep.tile([P, PACK * HALF], BF16, name="o_bf0", align_bytes=64)
        nc.scalar.copy(side_by_side(o_bf0[:], 2), by_runs(res[:, 0], 2))
        o_bf1 = keep.tile([P, PACK * HALF], BF16, name="o_bf1", align_bytes=64)
        nc.vector.tensor_copy(side_by_side(o_bf1[:], PACK), by_runs(res[:, 1], PACK))
        for rounded, (lo, hi) in zip((o_bf0, o_bf1), HALVES):
            nc.vector.quantize_mx(out=o_codes[:, lo:hi].bitcast(FP8X4), scales=o_scales[:, lo:hi], in_=rounded[:])
            nc.sync.dma_start(words_out[:, lo:hi], o_codes[:, lo:hi].bitcast(I32))
        scales_out = out_2[0].bitcast(I32)
        for q in range(QUADRANTS):
            queue = nc.scalar if q % 2 else nc.sync
            queue.dma_start(scales_out[4 * q : 4 * q + 4, :], o_scales[32 * q : 32 * q + 4, :].bitcast(I32))
